import numpy as np
CORES = [0,1,2,3,4,5,6,7,8,9,10,11,12,13,14,15,16,17,18,19,20,21,22,23,24,25,26,27,28,29,30,31,32,33,34,35,36,37,38,39,40,41,42,43,44,45,46,47,48,49,50,51,52,53,54,55,56,57,58,59,60,61,62,63]
N = 64
GROUPS = [[0,8,16,24,32,40,48,56],[1,9,17,25,33,41,49,57],[2,10,18,26,34,42,50,58],[3,11,19,27,35,43,51,59],[4,12,20,28,36,44,52,60],[5,13,21,29,37,45,53,61],[6,14,22,30,38,46,54,62],[7,15,23,31,39,47,55,63]]
def setup_inputs(rng):
    return {"x": rng.standard_normal((N, 128, 64), dtype=np.float32)}
def reference(x):
    y = np.empty((N, 128, 64), x.dtype)
    for g in GROUPS:
        s = x[g].sum(axis=0, dtype=np.float64).astype(x[g].dtype)
        for r in g:
            y[r] = s
    return {"y": y}

@@ -1,0 +1,73 @@
+from concourse.bass import DstId, RemoteDMATransfer
+
+PIECES = 4
+SCRATCH = {
+    "xs": ("dram", [4, 128, 16], "float32"),
+    "cb": ("dram", [8, 128, 16], "float32"),
+    "mb": ("dram", [2, 128, 16], "float32"),
+    "res": ("dram", [4, 128, 16], "float32"),
+}
+SEMAPHORES = ["ld", "sent", "c_arr", "m_arr", "r_arr"]
+
+SUMMER = {0: 2, 3: 2, 1: 3, 2: 3, 4: 6, 7: 6, 5: 7, 6: 7}
+SUMS = {2: (0, 3), 3: (1, 2), 6: (4, 7), 7: (5, 6)}
+
+
+def rank_program(g, core, T, topo):
+    rank = T.rank_of(core)
+    if rank is None:
+        return
+    chip, k = topo.chip(core), core % 8
+    q, pair = chip & 1, chip >> 1
+    sem = T.sem
+
+    def dst(c):
+        a = topo.addr(c)
+        return DstId(rid=a[0], pnc=a[1])
+
+    sent = 0
+
+    g.dma_start(T.xs[:], T.x[:]).then_inc(sem.ld, 16)
+    g.wait_ge(sem.ld, 16)
+
+    h = SUMMER[k]
+    slot = SUMS[h].index(k)
+    trs, off = [], 0
+    for m in range(PIECES):
+        to = (2 * m + q) * 8 + h
+        if m == pair:
+            mask = 0xFF00
+        else:
+            mask = 0x3 << (2 * off)
+            off += 1
+        trs.append(RemoteDMATransfer(dst_ids=[dst(to)], dma_engine_mask=mask, remote_sem=sem.c_arr,
+                                     src=T.xs[m], dst=T.cb[slot * 4 + pair]))
+        sent += 8 if m == pair else 2
+    g.remote_dma_fused(trs, local_sem=sem.sent)
+
+    if k in SUMS:
+        g.wait_ge(sem.c_arr, 2 * (3 * 2 + 8))
+        mate = (chip ^ 1) * 8 + k
+        trs = []
+        for s in range(2):
+            trs.append(RemoteDMATransfer(dst_ids=[dst(mate)], dma_engine_mask=0xF << (4 * s), remote_sem=sem.m_arr,
+                                         srcs=[T.cb[s * 4 + m] for m in range(4)], dsts=[T.mb[s]], alu_op=1))
+            sent += 4
+        g.remote_dma_fused(trs, local_sem=sem.sent)
+        g.wait_ge(sem.m_arr, 8)
+        trs = []
+        for s in range(2):
+            srcs = [T.cb[s * 4 + m] for m in range(4)] + [T.mb[s]]
+            far = [(2 * m + q) * 8 + SUMS[k][s] for m in range(PIECES) if m != pair]
+            near = chip * 8 + SUMS[k][s]
+            trs.append(RemoteDMATransfer(dst_ids=[dst(c) for c in far], dma_engine_mask=0xF << (4 * s),
+                                         remote_sem=sem.r_arr, srcs=srcs, dsts=[T.res[pair] for c in far], alu_op=1))
+            trs.append(RemoteDMATransfer(dst_ids=[dst(near)], dma_engine_mask=0xF00 << (4 * s),
+                                         remote_sem=sem.r_arr, srcs=srcs, dsts=[T.res[pair]], alu_op=1))
+            sent += 8
+        g.remote_dma_fused(trs, local_sem=sem.sent)
+
+    g.wait_ge(sem.r_arr, 16)
+    g.dma_start(T.y[:], T.res[:]).then_inc(sem.ld, 16)
+    g.wait_ge(sem.sent, sent)
+    g.wait_ge(sem.ld, 32)

@@ -4,13 +4,15 @@ PIECES = 4
 SCRATCH = {
     "xs": ("dram", [4, 128, 16], "float32"),
     "cb": ("dram", [8, 128, 16], "float32"),
-    "mb": ("dram", [2, 128, 16], "float32"),
+    "pb": ("dram", [2, 128, 16], "float32"),
     "res": ("dram", [4, 128, 16], "float32"),
 }
-SEMAPHORES = ["ld", "sent", "c_arr", "m_arr", "r_arr"]
+SEMAPHORES = ["ld", "sent", "c_arr", "p_arr", "r_arr"]
 
 SUMMER = {0: 2, 3: 2, 1: 3, 2: 3, 4: 6, 7: 6, 5: 7, 6: 7}
 SUMS = {2: (0, 3), 3: (1, 2), 6: (4, 7), 7: (5, 6)}
+FINISHER = {0: 3, 1: 2, 2: 0, 3: 1, 4: 7, 5: 6, 6: 4, 7: 5}
+FINISHES = {3: 0, 2: 1, 0: 2, 1: 3, 7: 4, 6: 5, 4: 6, 5: 7}
 
 
 def rank_program(g, core, T, topo):
@@ -47,27 +49,29 @@ def rank_program(g, core, T, topo):
 
     if k in SUMS:
         g.wait_ge(sem.c_arr, 2 * (3 * 2 + 8))
-        mate = (chip ^ 1) * 8 + k
         trs = []
         for s in range(2):
-            trs.append(RemoteDMATransfer(dst_ids=[dst(mate)], dma_engine_mask=0xF << (4 * s), remote_sem=sem.m_arr,
-                                         srcs=[T.cb[s * 4 + m] for m in range(4)], dsts=[T.mb[s]], alu_op=1))
-            sent += 4
-        g.remote_dma_fused(trs, local_sem=sem.sent)
-        g.wait_ge(sem.m_arr, 8)
-        trs = []
-        for s in range(2):
-            srcs = [T.cb[s * 4 + m] for m in range(4)] + [T.mb[s]]
-            far = [(2 * m + q) * 8 + SUMS[k][s] for m in range(PIECES) if m != pair]
-            near = chip * 8 + SUMS[k][s]
-            trs.append(RemoteDMATransfer(dst_ids=[dst(c) for c in far], dma_engine_mask=0xF << (4 * s),
-                                         remote_sem=sem.r_arr, srcs=srcs, dsts=[T.res[pair] for c in far], alu_op=1))
-            trs.append(RemoteDMATransfer(dst_ids=[dst(near)], dma_engine_mask=0xF00 << (4 * s),
-                                         remote_sem=sem.r_arr, srcs=srcs, dsts=[T.res[pair]], alu_op=1))
+            f = FINISHER[SUMS[k][s]]
+            srcs = [T.cb[s * 4 + m] for m in range(4)]
+            trs.append(RemoteDMATransfer(dst_ids=[dst((chip ^ 1) * 8 + f)], dma_engine_mask=0xF << (4 * s),
+                                         remote_sem=sem.p_arr, srcs=srcs, dsts=[T.pb[q]], alu_op=1))
+            trs.append(RemoteDMATransfer(dst_ids=[dst(chip * 8 + f)], dma_engine_mask=0xF00 << (4 * s),
+                                         remote_sem=sem.p_arr, srcs=srcs, dsts=[T.pb[q]], alu_op=1))
             sent += 8
         g.remote_dma_fused(trs, local_sem=sem.sent)
 
-    g.wait_ge(sem.r_arr, 16)
+    g.wait_ge(sem.p_arr, 8)
+    kk = FINISHES[k]
+    srcs = [T.pb[0], T.pb[1]]
+    far = [(2 * m + q) * 8 + kk for m in range(PIECES) if m != pair]
+    trs = [RemoteDMATransfer(dst_ids=[dst(c) for c in far], dma_engine_mask=0x00FF, remote_sem=sem.r_arr,
+                             srcs=srcs, dsts=[T.res[pair] for c in far], alu_op=1),
+           RemoteDMATransfer(dst_ids=[dst(chip * 8 + kk)], dma_engine_mask=0xFF00, remote_sem=sem.r_arr,
+                             srcs=srcs, dsts=[T.res[pair]], alu_op=1)]
+    sent += 16
+    g.remote_dma_fused(trs, local_sem=sem.sent)
+
+    g.wait_ge(sem.r_arr, 32)
     g.dma_start(T.y[:], T.res[:]).then_inc(sem.ld, 16)
     g.wait_ge(sem.sent, sent)
     g.wait_ge(sem.ld, 32)

@@ -1,13 +1,15 @@
 from concourse.bass import DstId, RemoteDMATransfer
 
 PIECES = 4
+CH = 2
+W = 16 // CH
 SCRATCH = {
-    "xs": ("dram", [4, 128, 16], "float32"),
-    "cb": ("dram", [8, 128, 16], "float32"),
-    "pb": ("dram", [2, 128, 16], "float32"),
-    "res": ("dram", [4, 128, 16], "float32"),
+    "xs": ("dram", [CH * 4, 128, W], "float32"),
+    "cb": ("dram", [CH * 8, 128, W], "float32"),
+    "pb": ("dram", [CH * 2, 128, W], "float32"),
+    "res": ("dram", [CH * 4, 128, W], "float32"),
 }
-SEMAPHORES = ["ld", "sent", "c_arr", "p_arr", "r_arr"]
+SEMAPHORES = ["ld", "sent", "c0", "c1", "p0", "p1", "r_arr"]
 
 SUMMER = {0: 2, 3: 2, 1: 3, 2: 3, 4: 6, 7: 6, 5: 7, 6: 7}
 SUMS = {2: (0, 3), 3: (1, 2), 6: (4, 7), 7: (5, 6)}
@@ -22,6 +24,8 @@ def rank_program(g, core, T, topo):
     chip, k = topo.chip(core), core % 8
     q, pair = chip & 1, chip >> 1
     sem = T.sem
+    c_arr = [sem.c0, sem.c1]
+    p_arr = [sem.p0, sem.p1]
 
     def dst(c):
         a = topo.addr(c)
@@ -34,44 +38,47 @@ def rank_program(g, core, T, topo):
 
     h = SUMMER[k]
     slot = SUMS[h].index(k)
-    trs, off = [], 0
-    for m in range(PIECES):
-        to = (2 * m + q) * 8 + h
-        if m == pair:
-            mask = 0xFF00
-        else:
-            mask = 0x3 << (2 * off)
-            off += 1
-        trs.append(RemoteDMATransfer(dst_ids=[dst(to)], dma_engine_mask=mask, remote_sem=sem.c_arr,
-                                     src=T.xs[m], dst=T.cb[slot * 4 + pair]))
-        sent += 8 if m == pair else 2
-    g.remote_dma_fused(trs, local_sem=sem.sent)
-
-    if k in SUMS:
-        g.wait_ge(sem.c_arr, 2 * (3 * 2 + 8))
-        trs = []
-        for s in range(2):
-            f = FINISHER[SUMS[k][s]]
-            srcs = [T.cb[s * 4 + m] for m in range(4)]
-            trs.append(RemoteDMATransfer(dst_ids=[dst((chip ^ 1) * 8 + f)], dma_engine_mask=0xF << (4 * s),
-                                         remote_sem=sem.p_arr, srcs=srcs, dsts=[T.pb[q]], alu_op=1))
-            trs.append(RemoteDMATransfer(dst_ids=[dst(chip * 8 + f)], dma_engine_mask=0xF00 << (4 * s),
-                                         remote_sem=sem.p_arr, srcs=srcs, dsts=[T.pb[q]], alu_op=1))
-            sent += 8
+    for j in range(CH):
+        trs, off = [], 0
+        for m in range(PIECES):
+            to = (2 * m + q) * 8 + h
+            if m == pair:
+                mask = 0xFF00
+            else:
+                mask = 0x3 << (2 * off)
+                off += 1
+            trs.append(RemoteDMATransfer(dst_ids=[dst(to)], dma_engine_mask=mask, remote_sem=c_arr[j],
+                                         src=T.xs[j * 4 + m], dst=T.cb[j * 8 + slot * 4 + pair]))
+            sent += 8 if m == pair else 2
         g.remote_dma_fused(trs, local_sem=sem.sent)
 
-    g.wait_ge(sem.p_arr, 8)
-    kk = FINISHES[k]
-    srcs = [T.pb[0], T.pb[1]]
-    far = [(2 * m + q) * 8 + kk for m in range(PIECES) if m != pair]
-    trs = [RemoteDMATransfer(dst_ids=[dst(c) for c in far], dma_engine_mask=0x00FF, remote_sem=sem.r_arr,
-                             srcs=srcs, dsts=[T.res[pair] for c in far], alu_op=1),
-           RemoteDMATransfer(dst_ids=[dst(chip * 8 + kk)], dma_engine_mask=0xFF00, remote_sem=sem.r_arr,
-                             srcs=srcs, dsts=[T.res[pair]], alu_op=1)]
-    sent += 16
-    g.remote_dma_fused(trs, local_sem=sem.sent)
+    if k in SUMS:
+        for j in range(CH):
+            g.wait_ge(c_arr[j], 2 * (3 * 2 + 8))
+            trs = []
+            for s in range(2):
+                f = FINISHER[SUMS[k][s]]
+                srcs = [T.cb[j * 8 + s * 4 + m] for m in range(4)]
+                trs.append(RemoteDMATransfer(dst_ids=[dst((chip ^ 1) * 8 + f)], dma_engine_mask=0xF << (4 * s),
+                                             remote_sem=p_arr[j], srcs=srcs, dsts=[T.pb[j * 2 + q]], alu_op=1))
+                trs.append(RemoteDMATransfer(dst_ids=[dst(chip * 8 + f)], dma_engine_mask=0xF00 << (4 * s),
+                                             remote_sem=p_arr[j], srcs=srcs, dsts=[T.pb[j * 2 + q]], alu_op=1))
+                sent += 8
+            g.remote_dma_fused(trs, local_sem=sem.sent)
 
-    g.wait_ge(sem.r_arr, 32)
+    kk = FINISHES[k]
+    far = [(2 * m + q) * 8 + kk for m in range(PIECES) if m != pair]
+    for j in range(CH):
+        g.wait_ge(p_arr[j], 8)
+        srcs = [T.pb[j * 2], T.pb[j * 2 + 1]]
+        trs = [RemoteDMATransfer(dst_ids=[dst(c) for c in far], dma_engine_mask=0x00FF, remote_sem=sem.r_arr,
+                                 srcs=srcs, dsts=[T.res[j * 4 + pair] for c in far], alu_op=1),
+               RemoteDMATransfer(dst_ids=[dst(chip * 8 + kk)], dma_engine_mask=0xFF00, remote_sem=sem.r_arr,
+                                 srcs=srcs, dsts=[T.res[j * 4 + pair]], alu_op=1)]
+        sent += 16
+        g.remote_dma_fused(trs, local_sem=sem.sent)
+
+    g.wait_ge(sem.r_arr, 32 * CH)
     g.dma_start(T.y[:], T.res[:]).then_inc(sem.ld, 16)
     g.wait_ge(sem.sent, sent)
     g.wait_ge(sem.ld, 32)

from concourse.bass import DstId, RemoteDMATransfer

PIECES = 4
CH = 2
W = 16 // CH
SCRATCH = {
    "xs": ("dram", [CH * 4, 128, W], "float32"),
    "cb": ("dram", [CH * 8, 128, W], "float32"),
    "pb": ("dram", [CH * 2, 128, W], "float32"),
    "res": ("dram", [CH * 4, 128, W], "float32"),
}
SEMAPHORES = ["ld", "sent", "c0", "c1", "p0", "p1", "r_arr"]

SUMMER = {0: 2, 3: 2, 1: 3, 2: 3, 4: 6, 7: 6, 5: 7, 6: 7}
SUMS = {2: (0, 3), 3: (1, 2), 6: (4, 7), 7: (5, 6)}
FINISHER = {0: 3, 1: 2, 2: 0, 3: 1, 4: 7, 5: 6, 6: 4, 7: 5}
FINISHES = {3: 0, 2: 1, 0: 2, 1: 3, 7: 4, 6: 5, 4: 6, 5: 7}


def rank_program(g, core, T, topo):
    rank = T.rank_of(core)
    if rank is None:
        return
    chip, k = topo.chip(core), core % 8
    q, pair = chip & 1, chip >> 1
    sem = T.sem
    c_arr = [sem.c0, sem.c1]
    p_arr = [sem.p0, sem.p1]

    def dst(c):
        a = topo.addr(c)
        return DstId(rid=a[0], pnc=a[1])

    sent = 0

    g.dma_start(T.xs[:], T.x[:]).then_inc(sem.ld, 16)
    g.wait_ge(sem.ld, 16)

    h = SUMMER[k]
    slot = SUMS[h].index(k)
    for j in range(CH):
        trs, off = [], 0
        for m in range(PIECES):
            to = (2 * m + q) * 8 + h
            if m == pair:
                mask = 0xFF00
            else:
                mask = 0x3 << (2 * off)
                off += 1
            trs.append(RemoteDMATransfer(dst_ids=[dst(to)], dma_engine_mask=mask, remote_sem=c_arr[j],
                                         src=T.xs[j * 4 + m], dst=T.cb[j * 8 + slot * 4 + pair]))
            sent += 8 if m == pair else 2
        g.remote_dma_fused(trs, local_sem=sem.sent)

    if k in SUMS:
        for j in range(CH):
            g.wait_ge(c_arr[j], 2 * (3 * 2 + 8))
            trs = []
            for s in range(2):
                f = FINISHER[SUMS[k][s]]
                srcs = [T.cb[j * 8 + s * 4 + m] for m in range(4)]
                trs.append(RemoteDMATransfer(dst_ids=[dst((chip ^ 1) * 8 + f)], dma_engine_mask=0xF << (4 * s),
                                             remote_sem=p_arr[j], srcs=srcs, dsts=[T.pb[j * 2 + q]], alu_op=1))
                trs.append(RemoteDMATransfer(dst_ids=[dst(chip * 8 + f)], dma_engine_mask=0xF00 << (4 * s),
                                             remote_sem=p_arr[j], srcs=srcs, dsts=[T.pb[j * 2 + q]], alu_op=1))
                sent += 8
            g.remote_dma_fused(trs, local_sem=sem.sent)

    kk = FINISHES[k]
    far = [(2 * m + q) * 8 + kk for m in range(PIECES) if m != pair]
    for j in range(CH):
        g.wait_ge(p_arr[j], 8)
        srcs = [T.pb[j * 2], T.pb[j * 2 + 1]]
        trs = [RemoteDMATransfer(dst_ids=[dst(c) for c in far], dma_engine_mask=0x00FF, remote_sem=sem.r_arr,
                                 srcs=srcs, dsts=[T.res[j * 4 + pair] for c in far], alu_op=1),
               RemoteDMATransfer(dst_ids=[dst(chip * 8 + kk)], dma_engine_mask=0xFF00, remote_sem=sem.r_arr,
                                 srcs=srcs, dsts=[T.res[j * 4 + pair]], alu_op=1)]
        sent += 16
        g.remote_dma_fused(trs, local_sem=sem.sent)

    g.wait_ge(sem.r_arr, 32 * CH)
    g.dma_start(T.y[:], T.res[:]).then_inc(sem.ld, 16)
    g.wait_ge(sem.sent, sent)
    g.wait_ge(sem.ld, 32)
